import numpy as np
import ml_dtypes


def mxq(x, axis, fmt="e4m3"):
    dtype, down = {"e4m3": (ml_dtypes.float8_e4m3fn, 7), "e5m2": (ml_dtypes.float8_e5m2, 14)}[fmt]
    v = np.moveaxis(np.asarray(x, np.float32).astype(ml_dtypes.bfloat16).astype(np.float64), axis, -1)
    blocks = v.reshape(v.shape[:-1] + (-1, 32))
    amax = np.abs(blocks).max(-1, keepdims=True)
    byte = np.maximum(np.where(amax > 0, np.frexp(amax)[1] - 1 + 127, 0) - down, 1)
    scale = np.exp2(byte - 127.0)
    codes = (blocks / scale).astype(np.float32).astype(dtype).astype(np.float64)
    return np.moveaxis((codes * scale).reshape(v.shape), -1, axis)


WIDE = False


def mx_kscale(k):
    if not WIDE:
        return np.ones(k)
    levels = np.array([10, -10, 5, -5, 0])
    if k % 512:
        return np.exp2(np.random.permutation(np.resize(levels, k // 32))).repeat(32)
    a = np.empty((k // 512, 16))
    for p in range(k // 512):
        a[p, :8] = np.random.permutation(np.resize(levels, 8))
        for g in range(8):
            far = levels[np.abs(levels - a[p, g]) >= 10]
            a[p, g + 8] = far[np.random.randint(len(far))]
    return np.exp2(a.ravel()).repeat(32)


def f64(x):
    return np.asarray(x).astype(np.float64)


E2M1 = np.array([0.0, 0.5, 1.0, 1.5, 2.0, 3.0, 4.0, 6.0, -0.0, -0.5, -1.0, -1.5, -2.0, -3.0, -4.0, -6.0])


def pack_weight(w, fmt):
    k, n = w.shape
    w = f64(np.asarray(w, np.float32).astype(ml_dtypes.bfloat16)).reshape(k // 32, 32, n)
    amax = np.abs(w).max(1)
    if fmt == "e4m3":
        byte = np.frexp(amax)[1] - 1 + 127 - 7
    else:
        mant, ex = np.frexp(amax / 6.0)
        byte = np.where(mant > 0.5, ex, ex - 1) + 127
    byte = np.clip(np.where(amax > 0, byte, 1), 1, 254)
    scaled = (w * np.exp2(127.0 - byte)[:, None, :]).reshape(k, n).astype(np.float32)
    by_word = np.ascontiguousarray(scaled.reshape(k // 512, 128, 4, n).transpose(0, 1, 3, 2))
    if fmt == "e4m3":
        words = by_word.astype(ml_dtypes.float8_e4m3fn).view(np.uint8)
    else:
        c = by_word.astype(ml_dtypes.float4_e2m1fn).view(np.uint8) & 0xF
        words = (c[..., 0::2] | (c[..., 1::2] << 4)).reshape(k // 512, 128, 2 * n)
    return np.ascontiguousarray(words), np.ascontiguousarray(byte.astype(np.uint8).reshape(k // 512, 16, n))


def unpack_weight(words, scales, fmt):
    g, _, n = scales.shape
    words = np.ascontiguousarray(words).reshape(g, 128, n, -1)
    if fmt == "e4m3":
        vals = words.view(ml_dtypes.float8_e4m3fn).astype(np.float64)
    else:
        nib = np.empty((g, 128, n, 4), np.uint8)
        nib[..., 0::2] = words & 0xF
        nib[..., 1::2] = words >> 4
        vals = E2M1[nib]
    vals = vals * np.repeat(np.exp2(scales.astype(np.float64) - 127.0), 8, axis=1)[..., None]
    return vals.transpose(0, 1, 3, 2).reshape(g * 512, n)


def planes(y):
    n, m = y.shape
    v = y.astype(np.float32).astype(ml_dtypes.bfloat16).astype(np.float64).reshape(n // 32, 32, m)
    top = np.abs(v).max(1)
    byte = np.clip(np.where(top > 0, np.frexp(top)[1] - 1 + 127 - 7, 1), 1, 254)
    codes = (v * np.exp2(127.0 - byte)[:, None, :]).reshape(n, m).astype(np.float32).astype(ml_dtypes.float8_e4m3fn).view(np.uint8)
    words = codes.reshape(n // 512, 128, 4, m).transpose(0, 1, 3, 2)
    return np.ascontiguousarray(words), np.ascontiguousarray(byte.astype(np.uint8).reshape(n // 512, 16, m))


def silu(v):
    return v / (1.0 + np.exp(-np.maximum(v, -700.0)))


K, M, T = 512, 1536, 1536


def setup_inputs():
    n = np.random.standard_normal
    s = mx_kscale(K)[:, None]
    p_w4 = pack_weight(n((K, M)) / np.sqrt(K) / s ** 2, "e2m1")
    p_w8 = pack_weight(n((K, M)) / np.sqrt(K) / s, "e4m3")
    return {
        "x": (n((K, T)) * s).astype(np.float32),
        "w4_words": p_w4[0],
        "w4_scales": p_w4[1],
        "w8_words": p_w8[0],
        "w8_scales": p_w8[1],
        "b": (0.3 * n(1536)).astype(np.float32),
    }


def reference(x, w4_words, w4_scales, w8_words, w8_scales, b):
    xa_, xb_ = mxq(f64(x) ** 2, 0, "e4m3"), mxq(f64(x), 0, "e4m3")
    w4_ = unpack_weight(w4_words, w4_scales, "e2m1")
    w8_ = unpack_weight(w8_words, w8_scales, "e4m3")
    y = xa_.T @ w4_ + xb_.T @ w8_
    out_0 = silu(y + f64(b)[None, :])
    return (out_0,) + planes(out_0)

from contextlib import ExitStack

import concourse.mybir as mybir
from concourse.masks import make_identity

K, M, T = 512, 1536, 1536
FLOPS = 2 * 2 * K * M * T

F32 = mybir.dt.float32
BF16 = mybir.dt.bfloat16
I32 = mybir.dt.int32
U8 = mybir.dt.uint8
FP8X4 = mybir.dt.float8_e4m3fn_x4
FP4X4 = mybir.dt.float4_e2m1fn_x4
ALU = mybir.AluOpType
ACT = mybir.ActivationFunctionType

P = 128
PACK = 4
CH = 512
NCH = 3
G_COLS = 352


def tile_mix_feat_tm_quadpl_silu_kernel(tc, x, w4_words, w4_scales, w8_words, w8_scales, b, out_0, out_1, out_2):
    nc = tc.nc
    x_v = x.rearrange("(p j) t -> p j t", j=PACK)
    w8_v = w8_words[0].rearrange("p n t -> p (n t)")
    w4_v = w4_words[0]
    out_v = out_0.rearrange("(a p i) n -> a p i n", p=P, i=PACK)

    with ExitStack() as ctx:
        keep = ctx.enter_context(tc.tile_pool(name="keep", bufs=1))
        work = ctx.enter_context(tc.tile_pool(name="work", bufs=1))
        psum = ctx.enter_context(tc.psum_pool(name="psum", bufs=8))
        ctx.enter_context(tc.manual_schedule())

        s8 = keep.tile([P, M], U8, align_bytes=64)
        s4 = keep.tile([P, M], U8, align_bytes=64)
        zero_in = keep.tile([P, 1], F32)
        zero = keep.tile([P, 1], F32)
        ident = keep.tile([P, P], F32)
        bcol = keep.tile([P, NCH, 8], F32)
        bias = [keep.tile([P, CH], F32, name="bias%d" % g) for g in range(NCH)]
        w8 = [keep.tile([P, CH], I32, name="w8_%d" % g, align_bytes=64) for g in range(NCH)]
        w4 = [keep.tile([P, 2 * CH], U8, name="w4_%d" % g, align_bytes=64) for g in range(NCH)]
        pieces = [2, 1, 1]
        xraw = [[keep.tile([P, PACK, CH // pieces[a]], F32, name="x%d_%d" % (a, h)) for h in range(pieces[a])] for a in range(NCH)]
        xb_codes = [keep.tile([P, CH], I32, name="xbc%d" % a, align_bytes=64) for a in range(NCH)]
        xa_codes = [keep.tile([P, CH], I32, name="xac%d" % a, align_bytes=64) for a in range(NCH)]
        xb_scales = [keep.tile([P, CH], U8, name="xbs%d" % a, align_bytes=64) for a in range(NCH)]
        xa_scales = [keep.tile([P, CH], U8, name="xas%d" % a, align_bytes=64) for a in range(NCH)]
        xb_bf = [keep.tile([P, PACK, P, PACK], BF16, name="xbb%d" % a, align_bytes=64) for a in range(NCH)]
        xa_bf = [keep.tile([P, PACK, P, PACK], BF16, name="xab%d" % a, align_bytes=64) for a in range(NCH)]
        early_scales = keep.tile([P, NCH - 1, M], U8, align_bytes=64)
        late_scales = keep.tile([P, 1, M], U8, align_bytes=64)
        out_scales = [early_scales[:, 0, :], early_scales[:, 1, :], late_scales[:, 0, :]]

        def load_x(a):
            w = CH // pieces[a]
            for h in range(pieces[a]):
                nc.sync.dma_start(out=xraw[a][h][:], in_=x_v[:, :, a * CH + h * w : a * CH + (h + 1) * w])

        def load_w8(g):
            nc.sync.dma_start(out=w8[g][:], in_=w8_v[:, 4 * CH * g : 4 * CH * (g + 1)].bitcast(I32))

        def load_w4(g):
            nc.sync.dma_start(out=w4[g][:].bitcast(I32), in_=w4_v[:, 2 * CH * g : 2 * CH * (g + 1)].bitcast(I32))

        def load_scales(eng, plane, rows):
            for q in range(4):
                eng.dma_start(out=plane[32 * q : 32 * q + 4, :].bitcast(I32), in_=rows[0, 4 * q : 4 * q + 4, :].bitcast(I32))

        def x_half(a, h):
            if pieces[a] == 2:
                return xraw[a][h][:].rearrange("p j (m r) -> p m j r", r=PACK)
            return xraw[a][0][:, :, h * 256 : (h + 1) * 256].rearrange("p j (m r) -> p m j r", r=PACK)

        def round_x(a, h):
            m0 = h * (P // pieces[a])
            m1 = m0 + P // pieces[a]
            nc.vector.tensor_copy(
                out=xb_bf[a][:, :, m0:m1, :].rearrange("p r m j -> p m j r"),
                in_=xraw[a][h][:].rearrange("p j (m r) -> p m j r", r=PACK),
            )

        def square_x(a, h):
            nc.scalar.activation(
                out=xa_bf[a][:, :, 64 * h : 64 * (h + 1), :].rearrange("p r m j -> p m j r"),
                in_=x_half(a, h), func=ACT.Square, bias=zero[:],
            )

        def quantize(codes, scales, src):
            nc.vector.quantize_mx(out=codes.bitcast(FP8X4), scales=scales, in_=src)

        def quantize_x(a):
            quantize(xb_codes[a][:], xb_scales[a][:], xb_bf[a][:].rearrange("p r m j -> p (r m j)"))
            quantize(xa_codes[a][:], xa_scales[a][:], xa_bf[a][:].rearrange("p r m j -> p (r m j)"))

        def multiply(a, g):
            banks = []
            for i in range(PACK):
                acc = psum.tile([P, CH], F32, tag="bank", name="acc")
                cols = slice(P * i, P * (i + 1))
                ncols = slice(CH * g, CH * (g + 1))
                nc.tensor.matmul_mx(out=acc[:], lhsT=xb_codes[a][:, cols].bitcast(FP8X4), lhsT_scale=xb_scales[a][:, cols],
                                    rhs=w8[g][:].bitcast(FP8X4), rhs_scale=s8[:, ncols], start=True, stop=False)
                nc.tensor.matmul_mx(out=acc[:], lhsT=xa_codes[a][:, cols].bitcast(FP8X4), lhsT_scale=xa_scales[a][:, cols],
                                    rhs=w4[g][:].bitcast(FP4X4), rhs_scale=s4[:, ncols], start=False, stop=True)
                banks.append(acc)
            return banks

        def add_bias(banks, g, c0, w):
            pre = []
            for i in range(PACK):
                f = work.tile([P, w], F32, tag="pre", name="pre", bufs=8)
                nc.vector.tensor_tensor(out=f[:], in0=banks[i][:, c0 : c0 + w], in1=bias[g][:, c0 : c0 + w], op=ALU.add)
                pre.append(f)
            return pre

        def silu(pre, w):
            o = work.tile([P, PACK, w], F32, tag="o", name="o", bufs=5)
            for i in range(PACK):
                nc.scalar.activation(out=o[:, i, :], in_=pre[i][:], func=ACT.Silu, bias=zero[:])
            return o

        def views(stage, o, c0, c1):
            return (stage[:, c0:c1, :].rearrange("p (c u) i -> p c i u", u=4),
                    o[:, :, c0:c1].rearrange("p i (c u) -> p c i u", u=4))

        def round_out(o, w, split, first):
            stage = work.tile([P, w, PACK], BF16, tag="stage", name="stage", bufs=1, align_bytes=64)
            dst, src = views(stage, o, 0, split)
            if first == "gpsimd":
                nc.gpsimd.tensor_scalar(out=dst, in0=src, scalar1=1.0, scalar2=-0.0, op0=ALU.mult, op1=ALU.add)
            else:
                nc.vector.tensor_copy(out=dst, in_=src)
            dst, src = views(stage, o, split, w)
            nc.scalar.copy(out=dst, in_=src)
            return stage

        def quantize_out(stage, a, n0, w):
            words = work.tile([P, w], I32, tag="words", name="words", bufs=4, align_bytes=64)
            quantize(words[:], out_scales[a][:, n0 : n0 + w], stage[:].rearrange("p n i -> p (n i)"))
            nc.sync.dma_start(out=out_1[a].rearrange("p n i -> p (n i)")[:, 4 * n0 : 4 * (n0 + w)].bitcast(I32), in_=words[:])

        def store_scales(planes, a0, a1, engines):
            for q in range(4):
                engines[q % len(engines)].dma_start(
                    out=out_2[a0:a1, 4 * q : 4 * q + 4, :].rearrange("a r n -> r a n").bitcast(I32),
                    in_=planes[32 * q : 32 * q + 4, :, :].bitcast(I32))

        nc.vector.memset(zero_in[:], 0.0)
        nc.vector.memset(s8[:].bitcast(I32), 0)
        nc.vector.memset(s4[:].bitcast(I32), 0)
        make_identity(nc, ident[:])
        nc.sync.dma_start(out=bcol[:, :, 0:PACK], in_=b.rearrange("(g p j) -> p g j", p=P, j=PACK))
        load_x(0)
        load_w8(0)
        load_scales(nc.sync, s8, w8_scales)
        nc.scalar.activation(out=zero[:], in_=zero_in[:], func=ACT.Silu)
        load_scales(nc.sync, s4, w4_scales)
        load_w4(0)
        load_x(1)
        for g in (1, 2):
            load_w8(g)
            load_w4(g)
        load_x(2)

        spread = []
        for g in range(NCH):
            ps = psum.tile([P, CH], F32, tag="bank", name="spread")
            for j in range(PACK):
                nc.tensor.transpose(ps[:, P * j : P * (j + 1)], bcol[:, g, j : j + 1].to_broadcast([P, P]), ident[:])
            spread.append(ps)
        for h in range(2):
            round_x(0, h)
            square_x(0, h)
        quantize_x(0)
        for g in range(NCH):
            nc.scalar.copy(out=bias[g][:].rearrange("q (p j) -> q p j", j=PACK), in_=spread[g][:].rearrange("q (j p) -> q p j", j=PACK))

        steps = [(a, g, 0, CH) for a in range(NCH) for g in range(NCH)][:-1]
        steps = steps + [(2, 2, 0, 256), (2, 2, 256, 256)]
        banks = {(0, 0): multiply(0, 0)}
        pending = None
        for s, (a, g, c0, w) in enumerate(steps):
            nxt = divmod(NCH * a + g + 1, NCH)
            if c0 == 0 and nxt[0] < NCH:
                banks[nxt] = multiply(*nxt)
            prep = a + 1 < NCH
            pre = add_bias(banks[(a, g)], g, c0, w)
            if prep and g == 1:
                square_x(a + 1, 1)
            o = silu(pre, w)
            nc.sync.dma_start(out=out_v[a, :, :, CH * g + c0 : CH * g + c0 + w], in_=o[:])
            if prep and g == 0:
                round_x(a + 1, 0)
                square_x(a + 1, 0)
            if prep and g == 1:
                quantize_x(a + 1)
            if pending is not None:
                quantize_out(*pending)
                if pending[1] == 1 and g == 0:
                    if a == 2:
                        store_scales(early_scales, 0, 2, [nc.sync])
            last = s == len(steps) - 1
            if last:
                stage = round_out(o, w, 160, "vector")
            else:
                stage = round_out(o, w, G_COLS * w // CH, "gpsimd")
            pending = (stage, a, CH * g + c0, w)
        quantize_out(*pending)
        store_scales(late_scales, 2, 3, [nc.scalar, nc.sync])
